import numpy as np
import ml_dtypes


def mxq(x, axis, fmt="e4m3"):
    dtype, down = {"e4m3": (ml_dtypes.float8_e4m3fn, 7), "e5m2": (ml_dtypes.float8_e5m2, 14)}[fmt]
    v = np.moveaxis(np.asarray(x, np.float32).astype(ml_dtypes.bfloat16).astype(np.float64), axis, -1)
    blocks = v.reshape(v.shape[:-1] + (-1, 32))
    amax = np.abs(blocks).max(-1, keepdims=True)
    byte = np.maximum(np.where(amax > 0, np.frexp(amax)[1] - 1 + 127, 0) - down, 1)
    scale = np.exp2(byte - 127.0)
    codes = (blocks / scale).astype(np.float32).astype(dtype).astype(np.float64)
    return np.moveaxis((codes * scale).reshape(v.shape), -1, axis)


WIDE = False


def mx_kscale(k):
    if not WIDE:
        return np.ones(k)
    levels = np.array([10, -10, 5, -5, 0])
    if k % 512:
        return np.exp2(np.random.permutation(np.resize(levels, k // 32))).repeat(32)
    a = np.empty((k // 512, 16))
    for p in range(k // 512):
        a[p, :8] = np.random.permutation(np.resize(levels, 8))
        for g in range(8):
            far = levels[np.abs(levels - a[p, g]) >= 10]
            a[p, g + 8] = far[np.random.randint(len(far))]
    return np.exp2(a.ravel()).repeat(32)


def f64(x):
    return np.asarray(x).astype(np.float64)


def striped(idx):
    return np.tile(idx.reshape(-1, 16).T, (8, 1)).astype(np.uint16)


def unstriped(offs):
    return offs[:16].T.reshape(-1).astype(np.int64)


def pack_weight(w):
    k, n = w.shape
    w = f64(np.asarray(w, np.float32).astype(ml_dtypes.bfloat16)).reshape(k // 32, 32, n)
    amax = np.abs(w).max(1)
    byte = np.clip(np.where(amax > 0, np.frexp(amax)[1] - 1 + 127 - 7, 1), 1, 254)
    scaled = (w * np.exp2(127.0 - byte)[:, None, :]).reshape(k, n).astype(np.float32)
    words = np.ascontiguousarray(scaled.reshape(k // 512, 128, 4, n).transpose(0, 1, 3, 2)).astype(ml_dtypes.float8_e4m3fn).view(np.uint8)
    return words, np.ascontiguousarray(byte.astype(np.uint8).reshape(k // 512, 16, n))


def unpack_weight(words, scales):
    g, p, n, _ = words.shape
    vals = np.ascontiguousarray(words).view(ml_dtypes.float8_e4m3fn).astype(np.float64) * np.repeat(np.exp2(scales.astype(np.float64) - 127.0), 8, axis=1)[..., None]
    return vals.transpose(0, 1, 3, 2).reshape(g * 512, n)


K, T, S, N, U = 512, 2048, 512, 128, 1024
P = 2 ** 7


def setup_inputs():
    n = np.random.standard_normal
    s = mx_kscale(K)[:, None]
    packed_xT = pack_weight(n((K, T)) * s)
    return {
        "x_words": packed_xT[0],
        "x_scales": packed_xT[1],
        "w1": (n((K, N)) / np.sqrt(K) / s).astype(np.float32),
        "ka": (np.tile(np.random.uniform(0.2, 1.0, U), (P, 1))).astype(np.float32),
        "kb": (np.tile(np.random.uniform(0.2, 1.0, U), (P, 1))).astype(np.float32),
        "iki": (np.tile(np.random.uniform(0.5, 2.0, U), (P, 1))).astype(np.float32),
        "vmax": (np.tile(np.random.uniform(0.5, 2.0, U), (P, 1))).astype(np.float32),
        "dil": (np.random.uniform(0.3, 1.0, (N, 1))).astype(np.float32),
        "offs": striped(np.random.permutation(T)[:S]),
        "suba": striped(np.random.permutation(np.concatenate([np.arange(S), np.random.randint(0, S, U - S)]))),
        "subb": striped(np.random.permutation(np.concatenate([np.arange(S), np.random.randint(0, S, U - S)]))),
        "inh": striped(np.random.permutation(np.concatenate([np.arange(S), np.random.randint(0, S, U - S)]))),
    }


def reference(x_words, x_scales, w1, ka, kb, iki, vmax, dil, offs, suba, subb, inh):
    xq = unpack_weight(x_words, x_scales)[:, unstriped(offs)]
    y = mxq(f64(w1), 0, "e4m3").T @ xq
    con = np.log(np.exp(y) + 1.0)
    cbb = con[:, unstriped(subb)]
    ci = con[:, unstriped(inh)]
    ca = con[:, unstriped(suba)]
    den = f64(kb)[:1] * ca + (f64(ka)[:1] * cbb) * (ci * f64(iki)[:1] + 1.0) + ca * cbb
    rate = ((ca * cbb) * f64(vmax)[:1]) / den
    return ((f64(ka)[:1] * cbb) * (ci * f64(iki)[:1] + 1.0)) / den - (f64(dil) * (rate / (ca + 0.3)))

@@ -1,0 +1,152 @@
+from contextlib import ExitStack
+
+import concourse.mybir as mybir
+
+F32 = mybir.dt.float32
+BF16 = mybir.dt.bfloat16
+I32 = mybir.dt.int32
+U32 = mybir.dt.uint32
+U16 = mybir.dt.uint16
+U8 = mybir.dt.uint8
+FP8X4 = mybir.dt.float8_e4m3fn_x4
+ALU = mybir.AluOpType
+ACT = mybir.ActivationFunctionType
+
+P = 128
+K, T, S, M, R = 512, 2048, 512, 128, 1024
+FLOPS = 2 * K * M * S
+HALF = S // 2
+WIN = S + 64
+WIDE = 2048
+LEAD = 512
+BIG = 2.0 ** 60
+TINY = 2.0 ** -60
+CH = 512
+
+
+def tile_picked_yppong_ela_p_kernel(
+    tc, x_words, x_scales, w1, ka, kb, iki, vmax, dil, offs, suba, subb, inh, out
+):
+    nc = tc.nc
+    with ExitStack() as ctx:
+        keep = ctx.enter_context(tc.tile_pool(name="keep", bufs=1))
+        psum = ctx.enter_context(tc.psum_pool(name="psum", bufs=1))
+
+        offs_t = keep.tile([P, S // 16], U16, name="offs_t")
+        suba_t = keep.tile([P, R // 16], U16, name="suba_t")
+        subb_t = keep.tile([P, R // 16], U16, name="subb_t")
+        inh_t = keep.tile([P, R // 16], U16, name="inh_t")
+        xs = keep.tile([P, T], U8, name="xs", align_bytes=64)
+        xw = keep.tile([P, T], I32, name="xw", align_bytes=64)
+        w_raw = keep.tile([P, 4, M], F32, name="w_raw")
+        warm = keep.tile([P, 8], F32, name="warm")
+        warm2 = keep.tile([P, 8], F32, name="warm2")
+
+        nc.vector.memset(xs[:].bitcast(I32), 0)
+        nc.vector.memset(warm[:], 0.0)
+        nc.scalar.activation(warm2[:], warm[:], ACT.Exp)
+
+        nc.sync.dma_start(w_raw[:], w1.rearrange("(p j) m -> p j m", j=4))
+        words = x_words[0].rearrange("p t r -> p (t r)").bitcast(I32)
+        nc.sync.dma_start(xw[:, 0:LEAD], words[:, 0:LEAD])
+        nc.sync.dma_start(offs_t[:], offs)
+        for q in range(4):
+            nc.sync.dma_start(xs[32 * q : 32 * q + 4, :].bitcast(I32), x_scales[0, 4 * q : 4 * q + 4, :].bitcast(I32))
+        nc.sync.dma_start(xw[:, LEAD:T], words[:, LEAD:T])
+        nc.sync.dma_start(inh_t[:], inh)
+        consts = {}
+        for name, src in (("iki", iki), ("ka", ka), ("kb", kb), ("vmax", vmax)):
+            consts[name] = keep.tile([P, R], F32, name=name + "_t")
+        nc.sync.dma_start(consts["iki"][:], iki)
+        nc.sync.dma_start(suba_t[:], suba)
+        nc.sync.dma_start(subb_t[:], subb)
+        nc.sync.dma_start(consts["ka"][:], ka)
+        nc.sync.dma_start(consts["kb"][:], kb)
+        nc.sync.dma_start(consts["vmax"][:], vmax)
+        dil_t = keep.tile([P, 1], F32, name="dil_t")
+        nc.sync.dma_start(dil_t[:], dil)
+
+        con = keep.tile([P, WIN], F32, name="con")
+        inv = keep.tile([P, WIN], F32, name="inv")
+        for t in (con, inv):
+            nc.gpsimd.memset(t[:, S:WIN], 0.0)
+        lc = keep.tile([P, WIDE], F32, name="lc")
+        lh = keep.tile([P, WIDE], F32, name="lh")
+        for t in (lc, lh):
+            nc.vector.memset(t[:, S:WIDE], 0.0)
+
+        w_bf = keep.tile([P, M, 4], BF16, name="w_bf", align_bytes=64)
+        w_codes = keep.tile([P, M], U32, name="w_codes", align_bytes=64)
+        w_scales = keep.tile([P, M], U8, name="w_scales", align_bytes=64)
+        nc.vector.tensor_copy(w_bf[:], w_raw[:].rearrange("p j m -> p m j"))
+        nc.vector.quantize_mx(
+            out=w_codes[:].bitcast(FP8X4), scales=w_scales[:], in_=w_bf[:].rearrange("p m j -> p (m j)")
+        )
+
+        gs = keep.tile([P, S], U8, name="gs", align_bytes=64)
+        nc.vector.tensor_copy(gs[:], xs[:].indirect(offs_t[:]))
+        ys, es = [], []
+        for h in range(2):
+            gw = keep.tile([P, HALF], U32, name=f"gw{h}", align_bytes=64)
+            nc.vector.tensor_copy(gw[:], xw[:].bitcast(U32).indirect(offs_t[:, 16 * h : 16 * (h + 1)]))
+            y = psum.tile([P, HALF], F32, name=f"y{h}")
+            nc.tensor.matmul_mx(
+                out=y[:], lhsT=w_codes[:].bitcast(FP8X4), lhsT_scale=w_scales[:],
+                rhs=gw[:].bitcast(FP8X4), rhs_scale=gs[:, HALF * h : HALF * (h + 1)], start=True, stop=True,
+            )
+            e = keep.tile([P, HALF], F32, name=f"e{h}")
+            nc.scalar.activation(e[:], y[:], ACT.Exp)
+            ys.append(y)
+            es.append(e)
+        ls = []
+        for h in range(2):
+            ec = keep.tile([P, HALF], F32, name=f"ec{h}")
+            nc.vector.tensor_scalar_min(ec[:], es[h][:], BIG)
+            ls.append(ec)
+        for h in range(2):
+            lg = keep.tile([P, HALF], F32, name=f"lg{h}")
+            nc.scalar.activation(lg[:], ls[h][:], ACT.Ln, bias=1.0)
+            nc.vector.scalar_tensor_tensor(
+                con[:, HALF * h : HALF * (h + 1)], lg[:], TINY, ys[h][:], ALU.max, ALU.max
+            )
+        for h in range(2):
+            hs = slice(HALF * h, HALF * (h + 1))
+            nc.scalar.activation(lc[:, hs], con[:, hs], ACT.Ln)
+        nc.scalar.activation(lh[:, 0:S], con[:, 0:S], ACT.Ln, bias=0.3)
+        nc.scalar.activation(inv[:, 0:S], lc[:, 0:S], ACT.Exp, scale=-1.0)
+
+        n = R // CH
+        cols = [slice(CH * c, CH * (c + 1)) for c in range(n)]
+        lcol = [slice(CH // 16 * c, CH // 16 * (c + 1)) for c in range(n)]
+
+        def tiles(name):
+            return [keep.tile([P, CH], F32, name=f"{name}{c}") for c in range(n)]
+
+        x, u, tt, yb, d, g, gv, nn, r1, r2, o = (
+            tiles(s) for s in ("x", "u", "tt", "yb", "d", "g", "gv", "nn", "ra", "rb", "o")
+        )
+        b0 = keep.tile([P, CH], F32, name="b0")
+        nc.scalar.activation(b0[:], lc[:].indirect(subb_t[:, lcol[0]]), ACT.Exp, scale=-1.0)
+        for c in range(n):
+            nc.scalar.activation(g[c][:], lh[:].indirect(suba_t[:, lcol[c]]), ACT.Exp, scale=-1.0)
+        for c in range(n):
+            nc.vector.tensor_tensor(x[c][:], con[:].indirect(inh_t[:, lcol[c]]), consts["iki"][:, cols[c]], ALU.mult)
+        for c in range(n):
+            nc.vector.scalar_tensor_tensor(u[c][:], x[c][:], 1.0, consts["ka"][:, cols[c]], ALU.add, ALU.mult)
+        for c in range(n):
+            nc.vector.tensor_tensor(tt[c][:], inv[:].indirect(suba_t[:, lcol[c]]), u[c][:], ALU.mult)
+        nc.vector.tensor_tensor(yb[1][:], inv[:].indirect(subb_t[:, lcol[1]]), consts["kb"][:, cols[1]], ALU.mult)
+        nc.vector.tensor_tensor(yb[0][:], b0[:], consts["kb"][:, cols[0]], ALU.mult)
+        for c in (1, 0):
+            nc.vector.scalar_tensor_tensor(d[c][:], yb[c][:], 1.0, tt[c][:], ALU.add, ALU.add)
+            nc.scalar.activation(r1[c][:], d[c][:], ACT.Abs_reciprocal_sqrt)
+            nc.scalar.activation(r2[c][:], r1[c][:], ACT.Square)
+        for c in (1, 0):
+            nc.vector.tensor_tensor(gv[c][:], g[c][:], consts["vmax"][:, cols[c]], ALU.mult)
+        for c in (1, 0):
+            nc.vector.scalar_tensor_tensor(nn[c][:], gv[c][:], dil_t[:], tt[c][:], ALU.mult, ALU.subtract)
+        for c in (1, 0):
+            for h in range(2):
+                hs = slice(HALF * h, HALF * (h + 1))
+                nc.vector.scalar_tensor_tensor(o[c][:, hs], nn[c][:, hs], -1.0, r2[c][:, hs], ALU.mult, ALU.mult)
+                nc.sync.dma_start(out[:, CH * c + HALF * h : CH * c + HALF * (h + 1)], o[c][:, hs])

@@ -1,6 +1,7 @@
 from contextlib import ExitStack
 
 import concourse.mybir as mybir
+from concourse.masks import make_identity
 
 F32 = mybir.dt.float32
 BF16 = mybir.dt.bfloat16
@@ -72,9 +73,10 @@ def tile_picked_yppong_ela_p_kernel(
             nc.gpsimd.memset(t[:, S:WIN], 0.0)
         lc = keep.tile([P, WIDE], F32, name="lc")
         lh = keep.tile([P, WIDE], F32, name="lh")
-        for t in (lc, lh):
-            nc.vector.memset(t[:, S:WIDE], 0.0)
+        nc.vector.memset(lh[:, S:WIDE], 0.0)
 
+        ident = keep.tile([P, P], F32, name="ident")
+        make_identity(nc, ident[:])
         w_bf = keep.tile([P, M, 4], BF16, name="w_bf", align_bytes=64)
         w_codes = keep.tile([P, M], U32, name="w_codes", align_bytes=64)
         w_scales = keep.tile([P, M], U8, name="w_scales", align_bytes=64)
@@ -94,20 +96,20 @@ def tile_picked_yppong_ela_p_kernel(
                 out=y[:], lhsT=w_codes[:].bitcast(FP8X4), lhsT_scale=w_scales[:],
                 rhs=gw[:].bitcast(FP8X4), rhs_scale=gs[:, HALF * h : HALF * (h + 1)], start=True, stop=True,
             )
-            e = keep.tile([P, HALF], F32, name=f"e{h}")
-            nc.scalar.activation(e[:], y[:], ACT.Exp)
+            e = lc[:, S + HALF * h : S + HALF * (h + 1)]
+            nc.scalar.activation(e, y[:], ACT.Exp)
             ys.append(y)
             es.append(e)
         ls = []
         for h in range(2):
-            ec = keep.tile([P, HALF], F32, name=f"ec{h}")
-            nc.vector.tensor_scalar_min(ec[:], es[h][:], BIG)
+            ec = lc[:, 2 * S + HALF * h : 2 * S + HALF * (h + 1)]
+            nc.vector.tensor_scalar_min(ec, es[h], BIG)
             ls.append(ec)
         for h in range(2):
-            lg = keep.tile([P, HALF], F32, name=f"lg{h}")
-            nc.scalar.activation(lg[:], ls[h][:], ACT.Ln, bias=1.0)
+            lg = lc[:, 3 * S + HALF * h : 3 * S + HALF * (h + 1)]
+            nc.scalar.activation(lg, ls[h], ACT.Ln, bias=1.0)
             nc.vector.scalar_tensor_tensor(
-                con[:, HALF * h : HALF * (h + 1)], lg[:], TINY, ys[h][:], ALU.max, ALU.max
+                con[:, HALF * h : HALF * (h + 1)], lg, TINY, ys[h][:], ALU.max, ALU.max
             )
         for h in range(2):
             hs = slice(HALF * h, HALF * (h + 1))
@@ -115,38 +117,69 @@ def tile_picked_yppong_ela_p_kernel(
         nc.scalar.activation(lh[:, 0:S], con[:, 0:S], ACT.Ln, bias=0.3)
         nc.scalar.activation(inv[:, 0:S], lc[:, 0:S], ACT.Exp, scale=-1.0)
 
-        n = R // CH
-        cols = [slice(CH * c, CH * (c + 1)) for c in range(n)]
-        lcol = [slice(CH // 16 * c, CH // 16 * (c + 1)) for c in range(n)]
+        def full(name):
+            return keep.tile([P, R], F32, name=name)
 
-        def tiles(name):
-            return [keep.tile([P, CH], F32, name=f"{name}{c}") for c in range(n)]
+        def lst(t, a, b):
+            return t[:, a // 16 : b // 16]
 
-        x, u, tt, yb, d, g, gv, nn, r1, r2, o = (
-            tiles(s) for s in ("x", "u", "tt", "yb", "d", "g", "gv", "nn", "ra", "rb", "o")
-        )
-        b0 = keep.tile([P, CH], F32, name="b0")
-        nc.scalar.activation(b0[:], lc[:].indirect(subb_t[:, lcol[0]]), ACT.Exp, scale=-1.0)
-        for c in range(n):
-            nc.scalar.activation(g[c][:], lh[:].indirect(suba_t[:, lcol[c]]), ACT.Exp, scale=-1.0)
-        for c in range(n):
-            nc.vector.tensor_tensor(x[c][:], con[:].indirect(inh_t[:, lcol[c]]), consts["iki"][:, cols[c]], ALU.mult)
-        for c in range(n):
-            nc.vector.scalar_tensor_tensor(u[c][:], x[c][:], 1.0, consts["ka"][:, cols[c]], ALU.add, ALU.mult)
-        for c in range(n):
-            nc.vector.tensor_tensor(tt[c][:], inv[:].indirect(suba_t[:, lcol[c]]), u[c][:], ALU.mult)
-        nc.vector.tensor_tensor(yb[1][:], inv[:].indirect(subb_t[:, lcol[1]]), consts["kb"][:, cols[1]], ALU.mult)
-        nc.vector.tensor_tensor(yb[0][:], b0[:], consts["kb"][:, cols[0]], ALU.mult)
-        for c in (1, 0):
-            nc.vector.scalar_tensor_tensor(d[c][:], yb[c][:], 1.0, tt[c][:], ALU.add, ALU.add)
-            nc.scalar.activation(r1[c][:], d[c][:], ACT.Abs_reciprocal_sqrt)
-            nc.scalar.activation(r2[c][:], r1[c][:], ACT.Square)
-        for c in (1, 0):
-            nc.vector.tensor_tensor(gv[c][:], g[c][:], consts["vmax"][:, cols[c]], ALU.mult)
-        for c in (1, 0):
-            nc.vector.scalar_tensor_tensor(nn[c][:], gv[c][:], dil_t[:], tt[c][:], ALU.mult, ALU.subtract)
-        for c in (1, 0):
-            for h in range(2):
-                hs = slice(HALF * h, HALF * (h + 1))
-                nc.vector.scalar_tensor_tensor(o[c][:, hs], nn[c][:, hs], -1.0, r2[c][:, hs], ALU.mult, ALU.mult)
-                nc.sync.dma_start(out[:, CH * c + HALF * h : CH * c + HALF * (h + 1)], o[c][:, hs])
+        x, u, tt, yb, g, gv, o = (full(s) for s in ("x", "u", "tt", "yb", "g", "gv", "o"))
+
+        def turned_sum(name, a, b, parts):
+            bank = psum.tile([P, b - a], F32, name=name)
+            for c in range(a, b, P):
+                for i, part in enumerate(parts):
+                    nc.tensor.matmul(
+                        bank[:, c - a : c - a + P], part[:, c : c + P], ident[:],
+                        start=(i == 0), stop=(i == len(parts) - 1), is_transpose=True,
+                    )
+            return bank
+
+        def turned_back(name, src):
+            w = src.shape[1]
+            bank = psum.tile([P, w], F32, name=name)
+            for c in range(0, w, P):
+                nc.tensor.transpose(bank[:, c : c + P], src[:, c : c + P], ident[:])
+            return bank
+
+        halves = ((0, CH), (CH, R))
+        for a, b in halves:
+            nc.scalar.activation(g[:, a:b], lh[:].indirect(lst(suba_t, a, b)), ACT.Exp, scale=-1.0)
+        for a, b in halves:
+            nc.vector.tensor_tensor(x[:, a:b], con[:].indirect(lst(inh_t, a, b)), consts["iki"][:, a:b], ALU.mult)
+        for a, b in halves:
+            nc.vector.scalar_tensor_tensor(u[:, a:b], x[:, a:b], 1.0, consts["ka"][:, a:b], ALU.add, ALU.mult)
+
+        def gather_t(a, b):
+            nc.vector.tensor_tensor(tt[:, a:b], inv[:].indirect(lst(suba_t, a, b)), u[:, a:b], ALU.mult)
+
+        def gather_y(a, b):
+            nc.vector.tensor_tensor(yb[:, a:b], inv[:].indirect(lst(subb_t, a, b)), consts["kb"][:, a:b], ALU.mult)
+
+        Q = CH // 2
+        units = ((0, CH), (CH, CH + Q), (CH + Q, R))
+        sums = []
+        for k, (a, b) in enumerate(units):
+            if a % CH == 0:
+                gather_t(a, a + CH)
+            gather_y(a, b)
+            sums.append(turned_sum(f"dt{k}", a, b, (tt, yb)))
+        rbs = []
+        for k, (a, b) in enumerate(units):
+            rt = keep.tile([P, b - a], F32, name=f"rt{k}")
+            rq = keep.tile([P, b - a], F32, name=f"rq{k}")
+            nc.scalar.activation(rt[:], sums[k][:], ACT.Abs_reciprocal_sqrt, bias=1.0)
+            nc.scalar.activation(rq[:], rt[:], ACT.Square)
+            rbs.append(turned_back(f"rb{k}", rq[:]))
+        nn = full("nn")
+        for a, b in halves:
+            nc.vector.tensor_tensor(gv[:, a:b], g[:, a:b], consts["vmax"][:, a:b], ALU.mult)
+        for a, b in halves:
+            nc.vector.scalar_tensor_tensor(nn[:, a:b], gv[:, a:b], dil_t[:], tt[:, a:b], ALU.mult, ALU.subtract)
+        for k, (ua, ub) in enumerate(units):
+            for a in range(ua, ub, Q):
+                b = a + Q
+                nc.vector.scalar_tensor_tensor(
+                    o[:, a:b], nn[:, a:b], -1.0, rbs[k][:, a - ua : b - ua], ALU.mult, ALU.mult
+                )
+                nc.sync.dma_start(out[:, a:b], o[:, a:b])

@@ -14,15 +14,24 @@ ALU = mybir.AluOpType
 ACT = mybir.ActivationFunctionType
 
 P = 128
-K, T, S, M, R = 512, 2048, 512, 128, 1024
+K = 512
+T = 2048
+S = 512
+M = 128
+R = 1024
 FLOPS = 2 * K * M * S
-HALF = S // 2
-WIN = S + 64
-WIDE = 2048
-LEAD = 512
-BIG = 2.0 ** 60
-TINY = 2.0 ** -60
-CH = 512
+
+PACK = 4
+LIST_ROWS = 16
+PICK_HALF = S // 2
+HALF = R // 2
+QUARTER = R // 4
+VECTOR_WINDOW = S + 64
+SCALAR_WINDOW = 4 * HALF
+LEAD = 256
+EXP_CAP = 2.0**60
+CON_FLOOR = 2.0**-60
+TURNOVER_SHIFT = 0.3
 
 
 def tile_picked_yppong_ela_p_kernel(
@@ -33,51 +42,54 @@ def tile_picked_yppong_ela_p_kernel(
         keep = ctx.enter_context(tc.tile_pool(name="keep", bufs=1))
         psum = ctx.enter_context(tc.psum_pool(name="psum", bufs=1))
 
-        offs_t = keep.tile([P, S // 16], U16, name="offs_t")
-        suba_t = keep.tile([P, R // 16], U16, name="suba_t")
-        subb_t = keep.tile([P, R // 16], U16, name="subb_t")
-        inh_t = keep.tile([P, R // 16], U16, name="inh_t")
-        xs = keep.tile([P, T], U8, name="xs", align_bytes=64)
-        xw = keep.tile([P, T], I32, name="xw", align_bytes=64)
-        w_raw = keep.tile([P, 4, M], F32, name="w_raw")
-        warm = keep.tile([P, 8], F32, name="warm")
-        warm2 = keep.tile([P, 8], F32, name="warm2")
+        def floats(name, width):
+            return keep.tile([P, width], F32, name=name)
 
-        nc.vector.memset(xs[:].bitcast(I32), 0)
-        nc.vector.memset(warm[:], 0.0)
-        nc.scalar.activation(warm2[:], warm[:], ACT.Exp)
+        def entries(list_tile, a, b):
+            return list_tile[:, a // LIST_ROWS : b // LIST_ROWS]
 
-        nc.sync.dma_start(w_raw[:], w1.rearrange("(p j) m -> p j m", j=4))
+        offs_t = keep.tile([P, S // LIST_ROWS], U16, name="offs_t")
+        suba_t = keep.tile([P, R // LIST_ROWS], U16, name="suba_t")
+        subb_t = keep.tile([P, R // LIST_ROWS], U16, name="subb_t")
+        inh_t = keep.tile([P, R // LIST_ROWS], U16, name="inh_t")
+        all_scales = keep.tile([P, T], U8, name="all_scales", align_bytes=64)
+        all_words = keep.tile([P, T], I32, name="all_words", align_bytes=64)
+        w_raw = keep.tile([P, PACK, M], F32, name="w_raw")
+
+        nc.vector.memset(all_scales[:].bitcast(I32), 0)
+
+        nc.sync.dma_start(w_raw[:], w1.rearrange("(p j) m -> p j m", j=PACK))
         words = x_words[0].rearrange("p t r -> p (t r)").bitcast(I32)
-        nc.sync.dma_start(xw[:, 0:LEAD], words[:, 0:LEAD])
+        nc.sync.dma_start(all_words[:, 0:LEAD], words[:, 0:LEAD])
         nc.sync.dma_start(offs_t[:], offs)
-        for q in range(4):
-            nc.sync.dma_start(xs[32 * q : 32 * q + 4, :].bitcast(I32), x_scales[0, 4 * q : 4 * q + 4, :].bitcast(I32))
-        nc.sync.dma_start(xw[:, LEAD:T], words[:, LEAD:T])
+        for q in (0, 2, 1, 3):
+            nc.sync.dma_start(
+                all_scales[32 * q : 32 * q + 4, :].bitcast(I32), x_scales[0, 4 * q : 4 * q + 4, :].bitcast(I32)
+            )
+        nc.sync.dma_start(all_words[:, LEAD:T], words[:, LEAD:T])
         nc.sync.dma_start(inh_t[:], inh)
-        consts = {}
-        for name, src in (("iki", iki), ("ka", ka), ("kb", kb), ("vmax", vmax)):
-            consts[name] = keep.tile([P, R], F32, name=name + "_t")
-        nc.sync.dma_start(consts["iki"][:], iki)
+        iki_t, ka_t, kb_t, vmax_t = (floats(name, R) for name in ("iki_t", "ka_t", "kb_t", "vmax_t"))
+        nc.sync.dma_start(iki_t[:], iki)
         nc.sync.dma_start(suba_t[:], suba)
         nc.sync.dma_start(subb_t[:], subb)
-        nc.sync.dma_start(consts["ka"][:], ka)
-        nc.sync.dma_start(consts["kb"][:], kb)
-        nc.sync.dma_start(consts["vmax"][:], vmax)
-        dil_t = keep.tile([P, 1], F32, name="dil_t")
+        nc.sync.dma_start(ka_t[:], ka)
+        nc.sync.dma_start(kb_t[:], kb)
+        nc.sync.dma_start(vmax_t[:], vmax)
+        dil_t = floats("dil_t", 1)
         nc.sync.dma_start(dil_t[:], dil)
 
-        con = keep.tile([P, WIN], F32, name="con")
-        inv = keep.tile([P, WIN], F32, name="inv")
-        for t in (con, inv):
-            nc.gpsimd.memset(t[:, S:WIN], 0.0)
-        lc = keep.tile([P, WIDE], F32, name="lc")
-        lh = keep.tile([P, WIDE], F32, name="lh")
-        nc.vector.memset(lh[:, S:WIDE], 0.0)
+        con = floats("con", VECTOR_WINDOW)
+        inv_con = floats("inv_con", VECTOR_WINDOW)
+        for window in (con, inv_con):
+            nc.vector.memset(window[:, S:VECTOR_WINDOW], 0.0)
+        log_con = floats("log_con", SCALAR_WINDOW)
+        log_shifted = floats("log_shifted", SCALAR_WINDOW)
+        ident = floats("ident", P)
+        nc.vector.memset(ident[:], 0.0)
+        make_identity(nc, ident[:], nomemset=True)
+        nc.vector.memset(log_shifted[:, S:SCALAR_WINDOW], 0.0)
 
-        ident = keep.tile([P, P], F32, name="ident")
-        make_identity(nc, ident[:])
-        w_bf = keep.tile([P, M, 4], BF16, name="w_bf", align_bytes=64)
+        w_bf = keep.tile([P, M, PACK], BF16, name="w_bf", align_bytes=64)
         w_codes = keep.tile([P, M], U32, name="w_codes", align_bytes=64)
         w_scales = keep.tile([P, M], U8, name="w_scales", align_bytes=64)
         nc.vector.tensor_copy(w_bf[:], w_raw[:].rearrange("p j m -> p m j"))
@@ -85,101 +97,111 @@ def tile_picked_yppong_ela_p_kernel(
             out=w_codes[:].bitcast(FP8X4), scales=w_scales[:], in_=w_bf[:].rearrange("p m j -> p (m j)")
         )
 
-        gs = keep.tile([P, S], U8, name="gs", align_bytes=64)
-        nc.vector.tensor_copy(gs[:], xs[:].indirect(offs_t[:]))
-        ys, es = [], []
-        for h in range(2):
-            gw = keep.tile([P, HALF], U32, name=f"gw{h}", align_bytes=64)
-            nc.vector.tensor_copy(gw[:], xw[:].bitcast(U32).indirect(offs_t[:, 16 * h : 16 * (h + 1)]))
-            y = psum.tile([P, HALF], F32, name=f"y{h}")
+        picked_scales = keep.tile([P, S], U8, name="picked_scales", align_bytes=64)
+        nc.vector.tensor_copy(picked_scales[:], all_scales[:].indirect(offs_t[:]))
+        picks = ((0, PICK_HALF), (PICK_HALF, S))
+        exp_y, capped, log1p = (log_con[:, n * S : (n + 1) * S] for n in (1, 2, 3))
+        y_banks = []
+        for h, (a, b) in enumerate(picks):
+            picked_words = keep.tile([P, PICK_HALF], U32, name=f"picked_words{h}", align_bytes=64)
+            nc.vector.tensor_copy(picked_words[:], all_words[:].bitcast(U32).indirect(entries(offs_t, a, b)))
+            y = psum.tile([P, PICK_HALF], F32, name=f"y{h}")
             nc.tensor.matmul_mx(
-                out=y[:], lhsT=w_codes[:].bitcast(FP8X4), lhsT_scale=w_scales[:],
-                rhs=gw[:].bitcast(FP8X4), rhs_scale=gs[:, HALF * h : HALF * (h + 1)], start=True, stop=True,
+                out=y[:],
+                lhsT=w_codes[:].bitcast(FP8X4),
+                lhsT_scale=w_scales[:],
+                rhs=picked_words[:].bitcast(FP8X4),
+                rhs_scale=picked_scales[:, a:b],
+                start=True,
+                stop=True,
             )
-            e = lc[:, S + HALF * h : S + HALF * (h + 1)]
-            nc.scalar.activation(e, y[:], ACT.Exp)
-            ys.append(y)
-            es.append(e)
-        ls = []
-        for h in range(2):
-            ec = lc[:, 2 * S + HALF * h : 2 * S + HALF * (h + 1)]
-            nc.vector.tensor_scalar_min(ec, es[h], BIG)
-            ls.append(ec)
-        for h in range(2):
-            lg = lc[:, 3 * S + HALF * h : 3 * S + HALF * (h + 1)]
-            nc.scalar.activation(lg, ls[h], ACT.Ln, bias=1.0)
+            nc.scalar.activation(exp_y[:, a:b], y[:], ACT.Exp)
+            y_banks.append(y)
+
+        for a, b in picks:
+            nc.vector.tensor_scalar_min(capped[:, a:b], exp_y[:, a:b], EXP_CAP)
+        for y, (a, b) in zip(y_banks, picks):
+            nc.scalar.activation(log1p[:, a:b], capped[:, a:b], ACT.Ln, bias=1.0)
+            nc.vector.scalar_tensor_tensor(con[:, a:b], log1p[:, a:b], CON_FLOOR, y[:], ALU.max, ALU.max)
+
+        for a, b in picks:
+            nc.scalar.activation(log_con[:, a:b], con[:, a:b], ACT.Ln)
+        nc.scalar.activation(log_shifted[:, 0:S], con[:, 0:S], ACT.Ln, bias=TURNOVER_SHIFT)
+        nc.scalar.activation(inv_con[:, 0:S], log_con[:, 0:S], ACT.Exp, scale=-1.0)
+
+        inhibition, ka_apparent, bound, kb_term, inv_shifted, turnover, result = (
+            floats(name, R)
+            for name in ("inhibition", "ka_apparent", "bound", "kb_term", "inv_shifted", "turnover", "result")
+        )
+        halves = ((0, HALF), (HALF, R))
+        quarters = tuple((a, a + QUARTER) for a in range(0, R, QUARTER))
+
+        inv_cbb = floats("inv_cbb", HALF)
+        nc.scalar.activation(inv_cbb[:], log_con[:].indirect(entries(subb_t, 0, HALF)), ACT.Exp, scale=-1.0)
+        for a, b in halves:
+            nc.scalar.activation(
+                inv_shifted[:, a:b], log_shifted[:].indirect(entries(suba_t, a, b)), ACT.Exp, scale=-1.0
+            )
+
+        for a, b in halves:
+            nc.vector.tensor_tensor(inhibition[:, a:b], con[:].indirect(entries(inh_t, a, b)), iki_t[:, a:b], ALU.mult)
+        for a, b in halves:
             nc.vector.scalar_tensor_tensor(
-                con[:, HALF * h : HALF * (h + 1)], lg, TINY, ys[h][:], ALU.max, ALU.max
+                ka_apparent[:, a:b], inhibition[:, a:b], 1.0, ka_t[:, a:b], ALU.add, ALU.mult
             )
-        for h in range(2):
-            hs = slice(HALF * h, HALF * (h + 1))
-            nc.scalar.activation(lc[:, hs], con[:, hs], ACT.Ln)
-        nc.scalar.activation(lh[:, 0:S], con[:, 0:S], ACT.Ln, bias=0.3)
-        nc.scalar.activation(inv[:, 0:S], lc[:, 0:S], ACT.Exp, scale=-1.0)
 
-        def full(name):
-            return keep.tile([P, R], F32, name=name)
+        def gather_bound(a, b):
+            nc.vector.tensor_tensor(
+                bound[:, a:b], inv_con[:].indirect(entries(suba_t, a, b)), ka_apparent[:, a:b], ALU.mult
+            )
 
-        def lst(t, a, b):
-            return t[:, a // 16 : b // 16]
-
-        x, u, tt, yb, g, gv, o = (full(s) for s in ("x", "u", "tt", "yb", "g", "gv", "o"))
-
-        def turned_sum(name, a, b, parts):
+        def transposed_sum(name, a, b):
             bank = psum.tile([P, b - a], F32, name=name)
             for c in range(a, b, P):
-                for i, part in enumerate(parts):
+                for first, term in ((True, bound), (False, kb_term)):
                     nc.tensor.matmul(
-                        bank[:, c - a : c - a + P], part[:, c : c + P], ident[:],
-                        start=(i == 0), stop=(i == len(parts) - 1), is_transpose=True,
+                        bank[:, c - a : c - a + P],
+                        term[:, c : c + P],
+                        ident[:],
+                        start=first,
+                        stop=not first,
+                        is_transpose=True,
                     )
+            return bank[:]
+
+        def transposed_back(name, blocks):
+            bank = psum.tile([P, QUARTER], F32, name=name)
+            for c in range(0, QUARTER, P):
+                nc.tensor.transpose(bank[:, c : c + P], blocks[:, c : c + P], ident[:])
             return bank
 
-        def turned_back(name, src):
-            w = src.shape[1]
-            bank = psum.tile([P, w], F32, name=name)
-            for c in range(0, w, P):
-                nc.tensor.transpose(bank[:, c : c + P], src[:, c : c + P], ident[:])
-            return bank
+        gather_bound(0, HALF)
+        nc.vector.tensor_tensor(kb_term[:, 0:HALF], inv_cbb[:], kb_t[:, 0:HALF], ALU.mult)
+        sums = [transposed_sum(f"sum{n}", a, b) for n, (a, b) in enumerate(quarters[:2])]
+        gather_bound(HALF, R)
+        nc.vector.tensor_tensor(
+            kb_term[:, HALF:R], inv_con[:].indirect(entries(subb_t, HALF, R)), kb_t[:, HALF:R], ALU.mult
+        )
+        second_sum = floats("second_sum", HALF)
+        nc.vector.tensor_tensor(second_sum[:], kb_term[:, HALF:R], bound[:, HALF:R], ALU.add)
+        sums.extend([second_sum[:, 0:QUARTER], second_sum[:, QUARTER:HALF]])
 
-        halves = ((0, CH), (CH, R))
-        for a, b in halves:
-            nc.scalar.activation(g[:, a:b], lh[:].indirect(lst(suba_t, a, b)), ACT.Exp, scale=-1.0)
-        for a, b in halves:
-            nc.vector.tensor_tensor(x[:, a:b], con[:].indirect(lst(inh_t, a, b)), consts["iki"][:, a:b], ALU.mult)
-        for a, b in halves:
-            nc.vector.scalar_tensor_tensor(u[:, a:b], x[:, a:b], 1.0, consts["ka"][:, a:b], ALU.add, ALU.mult)
+        inv_den = []
+        for n, (a, b) in enumerate(quarters):
+            root = floats(f"root{n}", QUARTER)
+            square = floats(f"square{n}", QUARTER)
+            nc.scalar.activation(root[:], sums[n], ACT.Abs_reciprocal_sqrt, bias=1.0)
+            nc.scalar.activation(square[:], root[:], ACT.Square)
+            inv_den.append(transposed_back(f"back{n}", square[:]) if b <= HALF else square)
 
-        def gather_t(a, b):
-            nc.vector.tensor_tensor(tt[:, a:b], inv[:].indirect(lst(suba_t, a, b)), u[:, a:b], ALU.mult)
-
-        def gather_y(a, b):
-            nc.vector.tensor_tensor(yb[:, a:b], inv[:].indirect(lst(subb_t, a, b)), consts["kb"][:, a:b], ALU.mult)
-
-        Q = CH // 2
-        units = ((0, CH), (CH, CH + Q), (CH + Q, R))
-        sums = []
-        for k, (a, b) in enumerate(units):
-            if a % CH == 0:
-                gather_t(a, a + CH)
-            gather_y(a, b)
-            sums.append(turned_sum(f"dt{k}", a, b, (tt, yb)))
-        rbs = []
-        for k, (a, b) in enumerate(units):
-            rt = keep.tile([P, b - a], F32, name=f"rt{k}")
-            rq = keep.tile([P, b - a], F32, name=f"rq{k}")
-            nc.scalar.activation(rt[:], sums[k][:], ACT.Abs_reciprocal_sqrt, bias=1.0)
-            nc.scalar.activation(rq[:], rt[:], ACT.Square)
-            rbs.append(turned_back(f"rb{k}", rq[:]))
-        nn = full("nn")
+        minus_num = floats("minus_num", R)
         for a, b in halves:
-            nc.vector.tensor_tensor(gv[:, a:b], g[:, a:b], consts["vmax"][:, a:b], ALU.mult)
+            nc.vector.tensor_tensor(turnover[:, a:b], inv_shifted[:, a:b], vmax_t[:, a:b], ALU.mult)
         for a, b in halves:
-            nc.vector.scalar_tensor_tensor(nn[:, a:b], gv[:, a:b], dil_t[:], tt[:, a:b], ALU.mult, ALU.subtract)
-        for k, (ua, ub) in enumerate(units):
-            for a in range(ua, ub, Q):
-                b = a + Q
-                nc.vector.scalar_tensor_tensor(
-                    o[:, a:b], nn[:, a:b], -1.0, rbs[k][:, a - ua : b - ua], ALU.mult, ALU.mult
-                )
-                nc.sync.dma_start(out[:, a:b], o[:, a:b])
+            nc.vector.scalar_tensor_tensor(
+                minus_num[:, a:b], turnover[:, a:b], dil_t[:], bound[:, a:b], ALU.mult, ALU.subtract
+            )
+        for n in (0, 2, 1, 3):
+            a, b = quarters[n]
+            nc.vector.scalar_tensor_tensor(result[:, a:b], minus_num[:, a:b], -1.0, inv_den[n][:], ALU.mult, ALU.mult)
+            nc.sync.dma_start(out[:, a:b], result[:, a:b])

from contextlib import ExitStack

import concourse.mybir as mybir
from concourse.masks import make_identity

F32 = mybir.dt.float32
BF16 = mybir.dt.bfloat16
I32 = mybir.dt.int32
U32 = mybir.dt.uint32
U16 = mybir.dt.uint16
U8 = mybir.dt.uint8
FP8X4 = mybir.dt.float8_e4m3fn_x4
ALU = mybir.AluOpType
ACT = mybir.ActivationFunctionType

P = 128
K = 512
T = 2048
S = 512
M = 128
R = 1024
FLOPS = 2 * K * M * S

PACK = 4
LIST_ROWS = 16
PICK_HALF = S // 2
HALF = R // 2
QUARTER = R // 4
VECTOR_WINDOW = S + 64
SCALAR_WINDOW = 4 * HALF
LEAD = 256
EXP_CAP = 2.0**60
CON_FLOOR = 2.0**-60
TURNOVER_SHIFT = 0.3


def tile_picked_yppong_ela_p_kernel(
    tc, x_words, x_scales, w1, ka, kb, iki, vmax, dil, offs, suba, subb, inh, out
):
    nc = tc.nc
    with ExitStack() as ctx:
        keep = ctx.enter_context(tc.tile_pool(name="keep", bufs=1))
        psum = ctx.enter_context(tc.psum_pool(name="psum", bufs=1))

        def floats(name, width):
            return keep.tile([P, width], F32, name=name)

        def entries(list_tile, a, b):
            return list_tile[:, a // LIST_ROWS : b // LIST_ROWS]

        offs_t = keep.tile([P, S // LIST_ROWS], U16, name="offs_t")
        suba_t = keep.tile([P, R // LIST_ROWS], U16, name="suba_t")
        subb_t = keep.tile([P, R // LIST_ROWS], U16, name="subb_t")
        inh_t = keep.tile([P, R // LIST_ROWS], U16, name="inh_t")
        all_scales = keep.tile([P, T], U8, name="all_scales", align_bytes=64)
        all_words = keep.tile([P, T], I32, name="all_words", align_bytes=64)
        w_raw = keep.tile([P, PACK, M], F32, name="w_raw")

        nc.vector.memset(all_scales[:].bitcast(I32), 0)

        nc.sync.dma_start(w_raw[:], w1.rearrange("(p j) m -> p j m", j=PACK))
        words = x_words[0].rearrange("p t r -> p (t r)").bitcast(I32)
        nc.sync.dma_start(all_words[:, 0:LEAD], words[:, 0:LEAD])
        nc.sync.dma_start(offs_t[:], offs)
        for q in (0, 2, 1, 3):
            nc.sync.dma_start(
                all_scales[32 * q : 32 * q + 4, :].bitcast(I32), x_scales[0, 4 * q : 4 * q + 4, :].bitcast(I32)
            )
        nc.sync.dma_start(all_words[:, LEAD:T], words[:, LEAD:T])
        nc.sync.dma_start(inh_t[:], inh)
        iki_t, ka_t, kb_t, vmax_t = (floats(name, R) for name in ("iki_t", "ka_t", "kb_t", "vmax_t"))
        nc.sync.dma_start(iki_t[:], iki)
        nc.sync.dma_start(suba_t[:], suba)
        nc.sync.dma_start(subb_t[:], subb)
        nc.sync.dma_start(ka_t[:], ka)
        nc.sync.dma_start(kb_t[:], kb)
        nc.sync.dma_start(vmax_t[:], vmax)
        dil_t = floats("dil_t", 1)
        nc.sync.dma_start(dil_t[:], dil)

        con = floats("con", VECTOR_WINDOW)
        inv_con = floats("inv_con", VECTOR_WINDOW)
        for window in (con, inv_con):
            nc.vector.memset(window[:, S:VECTOR_WINDOW], 0.0)
        log_con = floats("log_con", SCALAR_WINDOW)
        log_shifted = floats("log_shifted", SCALAR_WINDOW)
        ident = floats("ident", P)
        nc.vector.memset(ident[:], 0.0)
        make_identity(nc, ident[:], nomemset=True)
        nc.vector.memset(log_shifted[:, S:SCALAR_WINDOW], 0.0)

        w_bf = keep.tile([P, M, PACK], BF16, name="w_bf", align_bytes=64)
        w_codes = keep.tile([P, M], U32, name="w_codes", align_bytes=64)
        w_scales = keep.tile([P, M], U8, name="w_scales", align_bytes=64)
        nc.vector.tensor_copy(w_bf[:], w_raw[:].rearrange("p j m -> p m j"))
        nc.vector.quantize_mx(
            out=w_codes[:].bitcast(FP8X4), scales=w_scales[:], in_=w_bf[:].rearrange("p m j -> p (m j)")
        )

        picked_scales = keep.tile([P, S], U8, name="picked_scales", align_bytes=64)
        nc.vector.tensor_copy(picked_scales[:], all_scales[:].indirect(offs_t[:]))
        picks = ((0, PICK_HALF), (PICK_HALF, S))
        exp_y, capped, log1p = (log_con[:, n * S : (n + 1) * S] for n in (1, 2, 3))
        y_banks = []
        for h, (a, b) in enumerate(picks):
            picked_words = keep.tile([P, PICK_HALF], U32, name=f"picked_words{h}", align_bytes=64)
            nc.vector.tensor_copy(picked_words[:], all_words[:].bitcast(U32).indirect(entries(offs_t, a, b)))
            y = psum.tile([P, PICK_HALF], F32, name=f"y{h}")
            nc.tensor.matmul_mx(
                out=y[:],
                lhsT=w_codes[:].bitcast(FP8X4),
                lhsT_scale=w_scales[:],
                rhs=picked_words[:].bitcast(FP8X4),
                rhs_scale=picked_scales[:, a:b],
                start=True,
                stop=True,
            )
            nc.scalar.activation(exp_y[:, a:b], y[:], ACT.Exp)
            y_banks.append(y)

        for a, b in picks:
            nc.vector.tensor_scalar_min(capped[:, a:b], exp_y[:, a:b], EXP_CAP)
        for y, (a, b) in zip(y_banks, picks):
            nc.scalar.activation(log1p[:, a:b], capped[:, a:b], ACT.Ln, bias=1.0)
            nc.vector.scalar_tensor_tensor(con[:, a:b], log1p[:, a:b], CON_FLOOR, y[:], ALU.max, ALU.max)

        for a, b in picks:
            nc.scalar.activation(log_con[:, a:b], con[:, a:b], ACT.Ln)
        nc.scalar.activation(log_shifted[:, 0:S], con[:, 0:S], ACT.Ln, bias=TURNOVER_SHIFT)
        nc.scalar.activation(inv_con[:, 0:S], log_con[:, 0:S], ACT.Exp, scale=-1.0)

        inhibition, ka_apparent, bound, kb_term, inv_shifted, turnover, result = (
            floats(name, R)
            for name in ("inhibition", "ka_apparent", "bound", "kb_term", "inv_shifted", "turnover", "result")
        )
        halves = ((0, HALF), (HALF, R))
        quarters = tuple((a, a + QUARTER) for a in range(0, R, QUARTER))

        inv_cbb = floats("inv_cbb", HALF)
        nc.scalar.activation(inv_cbb[:], log_con[:].indirect(entries(subb_t, 0, HALF)), ACT.Exp, scale=-1.0)
        for a, b in halves:
            nc.scalar.activation(
                inv_shifted[:, a:b], log_shifted[:].indirect(entries(suba_t, a, b)), ACT.Exp, scale=-1.0
            )

        for a, b in halves:
            nc.vector.tensor_tensor(inhibition[:, a:b], con[:].indirect(entries(inh_t, a, b)), iki_t[:, a:b], ALU.mult)
        for a, b in halves:
            nc.vector.scalar_tensor_tensor(
                ka_apparent[:, a:b], inhibition[:, a:b], 1.0, ka_t[:, a:b], ALU.add, ALU.mult
            )

        def gather_bound(a, b):
            nc.vector.tensor_tensor(
                bound[:, a:b], inv_con[:].indirect(entries(suba_t, a, b)), ka_apparent[:, a:b], ALU.mult
            )

        def transposed_sum(name, a, b):
            bank = psum.tile([P, b - a], F32, name=name)
            for c in range(a, b, P):
                for first, term in ((True, bound), (False, kb_term)):
                    nc.tensor.matmul(
                        bank[:, c - a : c - a + P],
                        term[:, c : c + P],
                        ident[:],
                        start=first,
                        stop=not first,
                        is_transpose=True,
                    )
            return bank[:]

        def transposed_back(name, blocks):
            bank = psum.tile([P, QUARTER], F32, name=name)
            for c in range(0, QUARTER, P):
                nc.tensor.transpose(bank[:, c : c + P], blocks[:, c : c + P], ident[:])
            return bank

        gather_bound(0, HALF)
        nc.vector.tensor_tensor(kb_term[:, 0:HALF], inv_cbb[:], kb_t[:, 0:HALF], ALU.mult)
        sums = [transposed_sum(f"sum{n}", a, b) for n, (a, b) in enumerate(quarters[:2])]
        gather_bound(HALF, R)
        nc.vector.tensor_tensor(
            kb_term[:, HALF:R], inv_con[:].indirect(entries(subb_t, HALF, R)), kb_t[:, HALF:R], ALU.mult
        )
        second_sum = floats("second_sum", HALF)
        nc.vector.tensor_tensor(second_sum[:], kb_term[:, HALF:R], bound[:, HALF:R], ALU.add)
        sums.extend([second_sum[:, 0:QUARTER], second_sum[:, QUARTER:HALF]])

        inv_den = []
        for n, (a, b) in enumerate(quarters):
            root = floats(f"root{n}", QUARTER)
            square = floats(f"square{n}", QUARTER)
            nc.scalar.activation(root[:], sums[n], ACT.Abs_reciprocal_sqrt, bias=1.0)
            nc.scalar.activation(square[:], root[:], ACT.Square)
            inv_den.append(transposed_back(f"back{n}", square[:]) if b <= HALF else square)

        minus_num = floats("minus_num", R)
        for a, b in halves:
            nc.vector.tensor_tensor(turnover[:, a:b], inv_shifted[:, a:b], vmax_t[:, a:b], ALU.mult)
        for a, b in halves:
            nc.vector.scalar_tensor_tensor(
                minus_num[:, a:b], turnover[:, a:b], dil_t[:], bound[:, a:b], ALU.mult, ALU.subtract
            )
        for n in (0, 2, 1, 3):
            a, b = quarters[n]
            nc.vector.scalar_tensor_tensor(result[:, a:b], minus_num[:, a:b], -1.0, inv_den[n][:], ALU.mult, ALU.mult)
            nc.sync.dma_start(out[:, a:b], result[:, a:b])
